import numpy as np
import ml_dtypes


def mxq(x, axis, fmt="e4m3"):
    dtype, down = {"e4m3": (ml_dtypes.float8_e4m3fn, 7), "e5m2": (ml_dtypes.float8_e5m2, 14)}[fmt]
    v = np.moveaxis(np.asarray(x, np.float32).astype(ml_dtypes.bfloat16).astype(np.float64), axis, -1)
    blocks = v.reshape(v.shape[:-1] + (-1, 32))
    amax = np.abs(blocks).max(-1, keepdims=True)
    byte = np.maximum(np.where(amax > 0, np.frexp(amax)[1] - 1 + 127, 0) - down, 1)
    scale = np.exp2(byte - 127.0)
    codes = (blocks / scale).astype(np.float32).astype(dtype).astype(np.float64)
    return np.moveaxis((codes * scale).reshape(v.shape), -1, axis)


WIDE = False


def mx_kscale(k):
    if not WIDE:
        return np.ones(k)
    levels = np.array([10, -10, 5, -5, 0])
    if k % 512:
        return np.exp2(np.random.permutation(np.resize(levels, k // 32))).repeat(32)
    a = np.empty((k // 512, 16))
    for p in range(k // 512):
        a[p, :8] = np.random.permutation(np.resize(levels, 8))
        for g in range(8):
            far = levels[np.abs(levels - a[p, g]) >= 10]
            a[p, g + 8] = far[np.random.randint(len(far))]
    return np.exp2(a.ravel()).repeat(32)


def f64(x):
    return np.asarray(x).astype(np.float64)


def striped(idx):
    return np.tile(np.asarray(idx).reshape(-1, 16).T, (8, 1)).astype(np.uint16)


def unstriped(offs):
    return offs[:16].T.reshape(-1).astype(np.int64)


E2M1 = np.array([0.0, 0.5, 1.0, 1.5, 2.0, 3.0, 4.0, 6.0, -0.0, -0.5, -1.0, -1.5, -2.0, -3.0, -4.0, -6.0])


def pack_weight(w, fmt):
    k, n = w.shape
    w = f64(np.asarray(w, np.float32).astype(ml_dtypes.bfloat16)).reshape(k // 32, 32, n)
    amax = np.abs(w).max(1)
    if fmt == "e4m3":
        byte = np.frexp(amax)[1] - 1 + 127 - 7
    else:
        mant, ex = np.frexp(amax / 6.0)
        byte = np.where(mant > 0.5, ex, ex - 1) + 127
    byte = np.clip(np.where(amax > 0, byte, 1), 1, 254)
    scaled = (w * np.exp2(127.0 - byte)[:, None, :]).reshape(k, n).astype(np.float32)
    by_word = np.ascontiguousarray(scaled.reshape(k // 512, 128, 4, n).transpose(0, 1, 3, 2))
    if fmt == "e4m3":
        words = by_word.astype(ml_dtypes.float8_e4m3fn).view(np.uint8)
    else:
        c = by_word.astype(ml_dtypes.float4_e2m1fn).view(np.uint8) & 0xF
        words = (c[..., 0::2] | (c[..., 1::2] << 4)).reshape(k // 512, 128, 2 * n)
    return np.ascontiguousarray(words), np.ascontiguousarray(byte.astype(np.uint8).reshape(k // 512, 16, n))


def unpack_weight(words, scales, fmt):
    g, _, n = scales.shape
    words = np.ascontiguousarray(words).reshape(g, 128, n, -1)
    if fmt == "e4m3":
        vals = words.view(ml_dtypes.float8_e4m3fn).astype(np.float64)
    else:
        nib = np.empty((g, 128, n, 4), np.uint8)
        nib[..., 0::2] = words & 0xF
        nib[..., 1::2] = words >> 4
        vals = E2M1[nib]
    vals = vals * np.repeat(np.exp2(scales.astype(np.float64) - 127.0), 8, axis=1)[..., None]
    return vals.transpose(0, 1, 3, 2).reshape(g * 512, n)


D, T, Q, V = 512, 1024, 256, 2048


def setup_inputs():
    n = np.random.standard_normal
    idx = np.random.permutation(T)[:Q]
    idx2 = np.random.permutation(T)[:Q]
    idx3 = np.random.permutation(T)[:Q]
    fd = mx_kscale(D)
    candp = pack_weight(n((D, V)) / fd[:, None], "e4m3")
    return {
        "ent": (n((D, T)) * 1 / np.sqrt(D)).astype(np.float32),
        "fsc": (np.random.uniform(0.5, 1.5, (D, 1)) * fd[:, None]).astype(np.float32),
        "cand_words": candp[0],
        "cand_scales": candp[1],
        "temp": (np.random.uniform(1.5, 3.0, (Q, 1))).astype(np.float32),
        "offs": striped(idx),
        "offs2": striped(idx2),
        "offs3": striped(idx3),
    }


def reference(ent, fsc, cand_words, cand_scales, temp, offs, offs2, offs3):
    idx = unstriped(offs)
    idx2 = unstriped(offs2)
    idx3 = unstriped(offs3)
    candu = unpack_weight(cand_words, cand_scales, "e4m3")
    sv = (f64(ent)[:, idx2] - f64(ent)[:, idx] + f64(ent)[:, idx3]) * f64(fsc)
    svq = mxq(sv, 0, "e4m3")
    a = svq.T @ candu
    s = a / f64(temp)
    p = np.exp(s - np.max(s, axis=1, keepdims=True))
    y = p / np.sum(p, axis=1, keepdims=True) * 2048.0
    return y

@@ -1,0 +1,127 @@
+from contextlib import ExitStack
+
+import concourse.mybir as mybir
+
+D, T, Q, V = 512, 1024, 256, 2048
+FLOPS = 2 * D * Q * V
+
+F32 = mybir.dt.float32
+BF16 = mybir.dt.bfloat16
+I32 = mybir.dt.int32
+U32 = mybir.dt.uint32
+U16 = mybir.dt.uint16
+U8 = mybir.dt.uint8
+FP8X4 = mybir.dt.float8_e4m3fn_x4
+ALU = mybir.AluOpType
+ACT = mybir.ActivationFunctionType
+AX = mybir.AxisListType
+
+P = 128
+PACK = 4
+HALVES = Q // P
+N_TILE = 512
+CHUNKS = V // N_TILE
+LIST_COLS = P // 16
+
+
+def tile_attend_analogies_kernel(tc, ent, fsc, cand_words, cand_scales, temp, offs, offs2, offs3, out):
+    nc = tc.nc
+    with ExitStack() as ctx:
+        keep = ctx.enter_context(tc.tile_pool(name="keep", bufs=1))
+        psum = ctx.enter_context(tc.psum_pool(name="psum", bufs=1))
+
+        planes = [keep.tile([P, T], F32, name=f"plane{t}") for t in range(PACK)]
+        first = keep.tile([P, Q // 16], U16)
+        second = keep.tile([P, Q // 16], U16)
+        third = keep.tile([P, Q // 16], U16)
+        fsc_sb = keep.tile([P, PACK], F32)
+        temp_sb = keep.tile([P, HALVES], F32)
+        cand_plane = keep.tile([P, N_TILE], U8, align_bytes=64)
+        cand_sb = [keep.tile([P, N_TILE], U32, name=f"cand{j}", align_bytes=64) for j in range(CHUNKS)]
+
+        ent_planes = ent.rearrange("(p t) c -> t p c", t=PACK)
+        nc.gpsimd.memset(cand_plane[:].bitcast(I32), 0)
+        nc.sync.dma_start(planes[0][:], ent_planes[0])
+        nc.sync.dma_start(second[:], offs2)
+        nc.sync.dma_start(first[:], offs)
+        nc.sync.dma_start(third[:], offs3)
+        nc.scalar.dma_start(fsc_sb[:], fsc.rearrange("(p t) o -> p (t o)", t=PACK))
+        with nc.allow_non_contiguous_dma(reason="one temperature a partition and half"):
+            nc.scalar.dma_start(temp_sb[:], temp.rearrange("(h p) o -> p (h o)", p=P))
+        for t in range(1, PACK):
+            nc.sync.dma_start(planes[t][:], ent_planes[t])
+        scale_words = cand_scales[0].bitcast(I32).rearrange("f (j c) -> j f c", j=CHUNKS)
+        for g in range(4):
+            nc.sync.dma_start(cand_plane[32 * g : 32 * g + 16, :].bitcast(I32), scale_words[:, 4 * g : 4 * g + 4, :])
+        words = cand_words[0].rearrange("p n t -> p (n t)").bitcast(I32)
+        for j in range(CHUNKS):
+            nc.sync.dma_start(cand_sb[j][:].bitcast(I32), words[:, j * N_TILE : (j + 1) * N_TILE])
+
+        warm = keep.tile([P, 1], F32)
+        nc.gpsimd.memset(warm[:], 0.0)
+        warm_out = keep.tile([P, 1], F32)
+        nc.scalar.activation(warm_out[:], warm[:], ACT.Exp)
+
+        neg_temp = keep.tile([P, HALVES], F32)
+        nc.gpsimd.tensor_scalar(neg_temp[:], temp_sb[:], -1.0, 0.0, ALU.mult, ALU.add)
+        neg_inv_temp = keep.tile([P, HALVES], F32)
+        nc.vector.reciprocal(neg_inv_temp[:], neg_temp[:])
+
+        picked = [keep.tile([P, P], F32, name=f"picked{lane}") for lane in range(2)]
+        diff = [keep.tile([P, P], F32, name=f"diff{lane}") for lane in range(2)]
+        grouped = [keep.tile([P, P, PACK], BF16, name=f"grouped{h}", align_bytes=64) for h in range(HALVES)]
+        codes = [keep.tile([P, P], U32, name=f"codes{h}", align_bytes=64) for h in range(HALVES)]
+        sv_plane = [keep.tile([P, P], U8, name=f"sv_plane{h}", align_bytes=64) for h in range(HALVES)]
+
+        def gather_pair(pair):
+            cols = [slice(h * LIST_COLS, (h + 1) * LIST_COLS) for t, h in pair]
+            for lane, (t, h) in enumerate(pair):
+                nc.vector.tensor_copy(picked[lane][:], planes[t][:].indirect(second[:, cols[lane]]))
+            for lane, (t, h) in enumerate(pair):
+                nc.vector.tensor_tensor(diff[lane][:], planes[t][:].indirect(first[:, cols[lane]]), picked[lane][:], ALU.subtract)
+            for lane, (t, h) in enumerate(pair):
+                sought = keep.tile([P, P], F32, name=f"sought{t}_{h}")
+                nc.vector.tensor_tensor(sought[:], planes[t][:].indirect(third[:, cols[lane]]), diff[lane][:], ALU.subtract)
+                nc.scalar.activation(grouped[h][:, :, t], sought[:], ACT.Copy, scale=fsc_sb[:, t : t + 1])
+
+        banks = {}
+
+        def score(h):
+            nc.vector.quantize_mx(out=codes[h][:].bitcast(FP8X4), scales=sv_plane[h][:], in_=grouped[h][:].rearrange("p q t -> p (q t)"))
+            for j in range(CHUNKS):
+                banks[h, j] = psum.tile([P, N_TILE], F32, name=f"bank{h}_{j}")
+                nc.tensor.matmul_mx(out=banks[h, j][:], lhsT=codes[h][:].bitcast(FP8X4), lhsT_scale=sv_plane[h][:],
+                                    rhs=cand_sb[j][:].bitcast(FP8X4), rhs_scale=cand_plane[4 * j : P, :], start=True, stop=True)
+
+        def softmax(h, scaler):
+            neg_max = keep.tile([P, CHUNKS], F32, name=f"neg_max{h}")
+            sums = keep.tile([P, CHUNKS], F32, name=f"sums{h}")
+            neg_row_max = keep.tile([P, 1], F32, name=f"neg_row_max{h}")
+            shift = keep.tile([P, CHUNKS], F32, name=f"shift{h}")
+            prob = []
+            for j in range(CHUNKS):
+                neg_s = keep.tile([P, N_TILE], F32, name=f"neg_s{h}_{j}")
+                nc.vector.tensor_scalar(neg_s[:], banks[h, j][:], neg_inv_temp[:, h : h + 1], None, ALU.mult, ALU.min, accum_out=neg_max[:, j : j + 1])
+                if j == CHUNKS - 1:
+                    nc.vector.tensor_reduce(neg_row_max[:], neg_max[:], AX.X, ALU.min)
+                    nc.scalar.activation(shift[:], neg_max[:], ACT.Exp, bias=neg_row_max[:], scale=-1.0)
+                prob.append(keep.tile([P, N_TILE], F32, name=f"prob{h}_{j}"))
+                nc.scalar.activation(prob[j][:], neg_s[:], ACT.Exp, bias=neg_max[:, j : j + 1], scale=-1.0, accum_out=sums[:, j : j + 1])
+            weighted = keep.tile([P, CHUNKS], F32, name=f"weighted{h}")
+            mean = keep.tile([P, 1], F32, name=f"mean{h}")
+            nc.vector.scalar_tensor_tensor(weighted[:], sums[:], 1.0 / V, shift[:], ALU.mult, ALU.mult, accum_out=mean[:])
+            inv_mean = keep.tile([P, 1], F32, name=f"inv_mean{h}")
+            nc.vector.reciprocal(inv_mean[:], mean[:])
+            for j in range(CHUNKS):
+                result = keep.tile([P, N_TILE], F32, name=f"result{h}_{j}")
+                scaler.tensor_scalar(result[:], prob[j][:], shift[:, j : j + 1], inv_mean[:], ALU.mult, ALU.mult)
+                nc.sync.dma_start(out[h * P : (h + 1) * P, j * N_TILE : (j + 1) * N_TILE], result[:])
+
+        gather_pair([(0, 0), (0, 1)])
+        gather_pair([(1, 0), (1, 1)])
+        gather_pair([(2, 0), (3, 0)])
+        score(0)
+        gather_pair([(2, 1), (3, 1)])
+        score(1)
+        softmax(0, nc.gpsimd)
+        softmax(1, nc.vector)

@@ -67,22 +67,26 @@ def tile_attend_analogies_kernel(tc, ent, fsc, cand_words, cand_scales, temp, of
         neg_inv_temp = keep.tile([P, HALVES], F32)
         nc.vector.reciprocal(neg_inv_temp[:], neg_temp[:])
 
-        picked = [keep.tile([P, P], F32, name=f"picked{lane}") for lane in range(2)]
-        diff = [keep.tile([P, P], F32, name=f"diff{lane}") for lane in range(2)]
+        picked = [keep.tile([P, P], F32, name=f"picked{lane}")[:] for lane in range(2)]
+        held = [keep.tile([P, P], F32, name=f"held{t}")[:] for t in range(PACK - 1)]
         grouped = [keep.tile([P, P, PACK], BF16, name=f"grouped{h}", align_bytes=64) for h in range(HALVES)]
         codes = [keep.tile([P, P], U32, name=f"codes{h}", align_bytes=64) for h in range(HALVES)]
         sv_plane = [keep.tile([P, P], U8, name=f"sv_plane{h}", align_bytes=64) for h in range(HALVES)]
 
-        def gather_pair(pair):
-            cols = [slice(h * LIST_COLS, (h + 1) * LIST_COLS) for t, h in pair]
-            for lane, (t, h) in enumerate(pair):
-                nc.vector.tensor_copy(picked[lane][:], planes[t][:].indirect(second[:, cols[lane]]))
-            for lane, (t, h) in enumerate(pair):
-                nc.vector.tensor_tensor(diff[lane][:], planes[t][:].indirect(first[:, cols[lane]]), picked[lane][:], ALU.subtract)
-            for lane, (t, h) in enumerate(pair):
-                sought = keep.tile([P, P], F32, name=f"sought{t}_{h}")
-                nc.vector.tensor_tensor(sought[:], planes[t][:].indirect(third[:, cols[lane]]), diff[lane][:], ALU.subtract)
-                nc.scalar.activation(grouped[h][:, :, t], sought[:], ACT.Copy, scale=fsc_sb[:, t : t + 1])
+        cols = [slice(h * LIST_COLS, (h + 1) * LIST_COLS) for h in range(HALVES)]
+
+        def pick(t, h, dst):
+            nc.vector.tensor_copy(dst, planes[t][:].indirect(second[:, cols[h]]))
+
+        def less(t, h, src, dst):
+            nc.vector.tensor_tensor(dst, planes[t][:].indirect(first[:, cols[h]]), src, ALU.subtract)
+
+        def finish(t, h, src, dst):
+            nc.vector.tensor_tensor(dst, planes[t][:].indirect(third[:, cols[h]]), src, ALU.subtract)
+            nc.scalar.activation(grouped[h][:, :, t], dst, ACT.Copy, scale=fsc_sb[:, t : t + 1])
+
+        def fresh(t, h):
+            return keep.tile([P, P], F32, name=f"sought{t}_{h}")[:]
 
         banks = {}
 
@@ -93,35 +97,75 @@ def tile_attend_analogies_kernel(tc, ent, fsc, cand_words, cand_scales, temp, of
                 nc.tensor.matmul_mx(out=banks[h, j][:], lhsT=codes[h][:].bitcast(FP8X4), lhsT_scale=sv_plane[h][:],
                                     rhs=cand_sb[j][:].bitcast(FP8X4), rhs_scale=cand_plane[4 * j : P, :], start=True, stop=True)
 
-        def softmax(h, scaler):
-            neg_max = keep.tile([P, CHUNKS], F32, name=f"neg_max{h}")
-            sums = keep.tile([P, CHUNKS], F32, name=f"sums{h}")
-            neg_row_max = keep.tile([P, 1], F32, name=f"neg_row_max{h}")
-            shift = keep.tile([P, CHUNKS], F32, name=f"shift{h}")
-            prob = []
-            for j in range(CHUNKS):
-                neg_s = keep.tile([P, N_TILE], F32, name=f"neg_s{h}_{j}")
-                nc.vector.tensor_scalar(neg_s[:], banks[h, j][:], neg_inv_temp[:, h : h + 1], None, ALU.mult, ALU.min, accum_out=neg_max[:, j : j + 1])
-                if j == CHUNKS - 1:
-                    nc.vector.tensor_reduce(neg_row_max[:], neg_max[:], AX.X, ALU.min)
-                    nc.scalar.activation(shift[:], neg_max[:], ACT.Exp, bias=neg_row_max[:], scale=-1.0)
-                prob.append(keep.tile([P, N_TILE], F32, name=f"prob{h}_{j}"))
-                nc.scalar.activation(prob[j][:], neg_s[:], ACT.Exp, bias=neg_max[:, j : j + 1], scale=-1.0, accum_out=sums[:, j : j + 1])
-            weighted = keep.tile([P, CHUNKS], F32, name=f"weighted{h}")
-            mean = keep.tile([P, 1], F32, name=f"mean{h}")
-            nc.vector.scalar_tensor_tensor(weighted[:], sums[:], 1.0 / V, shift[:], ALU.mult, ALU.mult, accum_out=mean[:])
-            inv_mean = keep.tile([P, 1], F32, name=f"inv_mean{h}")
-            nc.vector.reciprocal(inv_mean[:], mean[:])
-            for j in range(CHUNKS):
-                result = keep.tile([P, N_TILE], F32, name=f"result{h}_{j}")
-                scaler.tensor_scalar(result[:], prob[j][:], shift[:, j : j + 1], inv_mean[:], ALU.mult, ALU.mult)
-                nc.sync.dma_start(out[h * P : (h + 1) * P, j * N_TILE : (j + 1) * N_TILE], result[:])
+        neg_max, sums, shift, mean, inv_mean, prob = {}, {}, {}, {}, {}, {}
+        for h in range(HALVES):
+            sums[h] = keep.tile([P, CHUNKS], F32, name=f"sums{h}")
+            shift[h] = keep.tile([P, CHUNKS], F32, name=f"shift{h}")
+            inv_mean[h] = keep.tile([P, 1], F32, name=f"inv_mean{h}")
+        last = keep.tile([P, 8 + P], F32)
+        neg_max[0] = last[:, 6:10]
+        stats = keep.tile([P, 2 * CHUNKS], F32)
+        neg_max[1] = stats[:, 0:4]
+        sums[0] = stats[:, 3:7]
+        sums[1] = sums[1][:]
+        mean[1] = keep.tile([P, 1], F32, name="mean1")[:]
+        mean[0] = keep.tile([P, 1], F32, name="mean0")[:]
 
-        gather_pair([(0, 0), (0, 1)])
-        gather_pair([(1, 0), (1, 1)])
-        gather_pair([(2, 0), (3, 0)])
+        def exponentials(h, chunks):
+            for j in chunks:
+                neg_s = keep.tile([P, N_TILE], F32, name=f"neg_s{h}_{j}")
+                nc.vector.tensor_scalar(neg_s[:], banks[h, j][:], neg_inv_temp[:, h : h + 1], None, ALU.mult, ALU.min, accum_out=neg_max[h][:, j : j + 1])
+                if j == CHUNKS - 1:
+                    neg_row_max = keep.tile([P, 1], F32, name=f"neg_row_max{h}")
+                    if h == 0:
+                        partial = keep.tile([P, 1], F32)
+                        nc.gpsimd.tensor_scalar(partial[:], neg_max[h][:, 0:1], neg_max[h][:, 1:2], neg_max[h][:, 2:3], ALU.min, ALU.min)
+                        nc.gpsimd.tensor_scalar(neg_row_max[:], partial[:], neg_max[h][:, 3:4], None, ALU.min)
+                    else:
+                        nc.vector.tensor_reduce(neg_row_max[:], neg_max[h], AX.X, ALU.min)
+                    nc.scalar.activation(shift[h][:], neg_max[h], ACT.Exp, bias=neg_row_max[:], scale=-1.0)
+                prob[h, j] = keep.tile([P, N_TILE], F32, name=f"prob{h}_{j}")
+                nc.scalar.activation(prob[h, j][:], neg_s[:], ACT.Exp, bias=neg_max[h][:, j : j + 1], scale=-1.0, accum_out=sums[h][:, j : j + 1])
+
+        def normaliser(h):
+            weighted = keep.tile([P, CHUNKS], F32, name=f"weighted{h}")
+            nc.vector.scalar_tensor_tensor(weighted[:], sums[h], 1.0 / V, shift[h][:], ALU.mult, ALU.mult, accum_out=mean[h])
+            nc.vector.reciprocal(inv_mean[h][:], mean[h])
+
+        def emit(h, j, engine, pieces):
+            result = keep.tile([P, N_TILE], F32, name=f"result{h}_{j}")
+            for a, b in pieces:
+                engine.tensor_scalar(result[:, a:b], prob[h, j][:, a:b], shift[h][:, j : j + 1], inv_mean[h][:], ALU.mult, ALU.mult)
+                nc.sync.dma_start(out[h * P : (h + 1) * P, j * N_TILE + a : j * N_TILE + b], result[:, a:b])
+
+        row = keep.tile([P, 3 * P], F32)
+        diff0 = row[:, P : 2 * P]
+        for t in range(PACK):
+            pick(t, 0, picked[0])
+            if t < PACK - 1:
+                pick(t, 1, picked[1])
+            less(t, 0, picked[0], diff0)
+            if t < PACK - 1:
+                less(t, 1, picked[1], held[t])
+            sought = fresh(t, 0)
+            finish(t, 0, diff0, sought)
         score(0)
-        gather_pair([(2, 1), (3, 1)])
+        finish(0, 1, held[0], picked[0])
+        finish(1, 1, held[1], row[:, 8 : P + 8])
+        pick(3, 1, row[:, 2 * P - 8 : 3 * P - 8])
+        less(3, 1, row[:, 2 * P - 8 : 3 * P - 8], sought)
+        finish(2, 1, held[2], grouped[0][:].rearrange("p q t -> p (q t)").bitcast(F32)[:, :P])
+        finish(3, 1, sought, last[:, 8:])
+        exponentials(0, range(1))
         score(1)
-        softmax(0, nc.gpsimd)
-        softmax(1, nc.vector)
+        exponentials(0, range(1, CHUNKS))
+        exponentials(1, range(2))
+        normaliser(0)
+        emit(0, 0, nc.gpsimd, [(0, 128), (128, N_TILE)])
+        emit(0, 1, nc.gpsimd, [(0, N_TILE)])
+        exponentials(1, range(2, CHUNKS))
+        emit(0, 2, nc.vector, [(0, N_TILE)])
+        emit(0, 3, nc.vector, [(0, N_TILE)])
+        normaliser(1)
+        for j in range(CHUNKS):
+            emit(1, j, nc.vector, [(0, N_TILE)])

@@ -22,6 +22,11 @@ HALVES = Q // P
 N_TILE = 512
 CHUNKS = V // N_TILE
 LIST_COLS = P // 16
+PIECES = (
+    ((0, 256), (256, 256), (512, 512), (1024, 512), (1536, 512)),
+    ((0, 512), (512, 512), (1024, 512), (1536, 512)),
+)
+NP = 5
 
 
 def tile_attend_analogies_kernel(tc, ent, fsc, cand_words, cand_scales, temp, offs, offs2, offs3, out):
@@ -37,43 +42,50 @@ def tile_attend_analogies_kernel(tc, ent, fsc, cand_words, cand_scales, temp, of
         fsc_sb = keep.tile([P, PACK], F32)
         temp_sb = keep.tile([P, HALVES], F32)
         cand_plane = keep.tile([P, N_TILE], U8, align_bytes=64)
-        cand_sb = [keep.tile([P, N_TILE], U32, name=f"cand{j}", align_bytes=64) for j in range(CHUNKS)]
+        cand_sb = keep.tile([P, V], U32, align_bytes=64)
 
         ent_planes = ent.rearrange("(p t) c -> t p c", t=PACK)
-        nc.gpsimd.memset(cand_plane[:].bitcast(I32), 0)
+        nc.vector.memset(cand_plane[:].bitcast(I32), 0)
         nc.sync.dma_start(planes[0][:], ent_planes[0])
         nc.sync.dma_start(second[:], offs2)
         nc.sync.dma_start(first[:], offs)
         nc.sync.dma_start(third[:], offs3)
-        nc.scalar.dma_start(fsc_sb[:], fsc.rearrange("(p t) o -> p (t o)", t=PACK))
+        nc.sync.dma_start(planes[1][:], ent_planes[1])
+        nc.sync.dma_start(fsc_sb[:], fsc.rearrange("(p t) o -> p (t o)", t=PACK))
+        nc.sync.dma_start(planes[2][:], ent_planes[2])
+        nc.sync.dma_start(planes[3][:], ent_planes[3])
+        nc.sync.dma_start(cand_sb[:].bitcast(I32), cand_words[0].rearrange("p n t -> p (n t)").bitcast(I32))
         with nc.allow_non_contiguous_dma(reason="one temperature a partition and half"):
-            nc.scalar.dma_start(temp_sb[:], temp.rearrange("(h p) o -> p (h o)", p=P))
-        for t in range(1, PACK):
-            nc.sync.dma_start(planes[t][:], ent_planes[t])
+            nc.gpsimd.dma_start(temp_sb[:], temp.rearrange("(h p) o -> p (h o)", p=P))
         scale_words = cand_scales[0].bitcast(I32).rearrange("f (j c) -> j f c", j=CHUNKS)
         for g in range(4):
-            nc.sync.dma_start(cand_plane[32 * g : 32 * g + 16, :].bitcast(I32), scale_words[:, 4 * g : 4 * g + 4, :])
-        words = cand_words[0].rearrange("p n t -> p (n t)").bitcast(I32)
-        for j in range(CHUNKS):
-            nc.sync.dma_start(cand_sb[j][:].bitcast(I32), words[:, j * N_TILE : (j + 1) * N_TILE])
-
-        warm = keep.tile([P, 1], F32)
-        nc.gpsimd.memset(warm[:], 0.0)
-        warm_out = keep.tile([P, 1], F32)
-        nc.scalar.activation(warm_out[:], warm[:], ACT.Exp)
-
+            nc.gpsimd.dma_start(cand_plane[32 * g : 32 * g + 16, :].bitcast(I32), scale_words[:, 4 * g : 4 * g + 4, :])
         neg_temp = keep.tile([P, HALVES], F32)
         nc.gpsimd.tensor_scalar(neg_temp[:], temp_sb[:], -1.0, 0.0, ALU.mult, ALU.add)
         neg_inv_temp = keep.tile([P, HALVES], F32)
         nc.vector.reciprocal(neg_inv_temp[:], neg_temp[:])
 
+        warm = keep.tile([P, 1], F32)
+        nc.vector.memset(warm[:], 0.0)
+        warm_out = keep.tile([P, 1], F32)
+        nc.scalar.activation(warm_out[:], warm[:], ACT.Exp)
+
         picked = [keep.tile([P, P], F32, name=f"picked{lane}")[:] for lane in range(2)]
-        held = [keep.tile([P, P], F32, name=f"held{t}")[:] for t in range(PACK - 1)]
+        stats = keep.tile([P, 2 * NP], F32)
+        mixed = keep.tile([P, 2 * P + 8], F32)
+        held = [keep.tile([P, P], F32, name=f"held{t}")[:] for t in range(2)] + [mixed[:, :P]]
+        last = mixed[:, P + 8 :]
+        neg_max = [mixed[:, P - 1 : P + 20 : 5], stats[:, 0:CHUNKS]]
         grouped = [keep.tile([P, P, PACK], BF16, name=f"grouped{h}", align_bytes=64) for h in range(HALVES)]
         codes = [keep.tile([P, P], U32, name=f"codes{h}", align_bytes=64) for h in range(HALVES)]
         sv_plane = [keep.tile([P, P], U8, name=f"sv_plane{h}", align_bytes=64) for h in range(HALVES)]
-
+        sums = [stats[:, 2 : 2 + NP], keep.tile([P, CHUNKS], F32, name="sums1")[:]]
+        shift = [keep.tile([P, len(PIECES[h])], F32, name=f"shift{h}") for h in range(HALVES)]
+        mean = [keep.tile([P, 1], F32, name=f"mean{h}") for h in range(HALVES)]
+        inv_mean = [keep.tile([P, 1], F32, name=f"inv_mean{h}") for h in range(HALVES)]
+        neg_row_max = [keep.tile([P, 1], F32, name=f"neg_row_max{h}")[:] for h in range(HALVES)]
         cols = [slice(h * LIST_COLS, (h + 1) * LIST_COLS) for h in range(HALVES)]
+        banks, prob = {}, {}
 
         def pick(t, h, dst):
             nc.vector.tensor_copy(dst, planes[t][:].indirect(second[:, cols[h]]))
@@ -85,58 +97,46 @@ def tile_attend_analogies_kernel(tc, ent, fsc, cand_words, cand_scales, temp, of
             nc.vector.tensor_tensor(dst, planes[t][:].indirect(third[:, cols[h]]), src, ALU.subtract)
             nc.scalar.activation(grouped[h][:, :, t], dst, ACT.Copy, scale=fsc_sb[:, t : t + 1])
 
-        def fresh(t, h):
-            return keep.tile([P, P], F32, name=f"sought{t}_{h}")[:]
-
-        banks = {}
-
         def score(h):
             nc.vector.quantize_mx(out=codes[h][:].bitcast(FP8X4), scales=sv_plane[h][:], in_=grouped[h][:].rearrange("p q t -> p (q t)"))
-            for j in range(CHUNKS):
-                banks[h, j] = psum.tile([P, N_TILE], F32, name=f"bank{h}_{j}")
-                nc.tensor.matmul_mx(out=banks[h, j][:], lhsT=codes[h][:].bitcast(FP8X4), lhsT_scale=sv_plane[h][:],
-                                    rhs=cand_sb[j][:].bitcast(FP8X4), rhs_scale=cand_plane[4 * j : P, :], start=True, stop=True)
+            whole = [psum.tile([P, N_TILE], F32, name=f"bank{h}_{j}") for j in range(CHUNKS)]
+            for i, (start, width) in enumerate(PIECES[h]):
+                j, a = divmod(start, N_TILE)
+                banks[h, i] = whole[j][:, a : a + width]
+                nc.tensor.matmul_mx(out=banks[h, i], lhsT=codes[h][:].bitcast(FP8X4), lhsT_scale=sv_plane[h][:],
+                                    rhs=cand_sb[:, start : start + width].bitcast(FP8X4), rhs_scale=cand_plane[4 * j : P, a : a + width], start=True, stop=True)
 
-        neg_max, sums, shift, mean, inv_mean, prob = {}, {}, {}, {}, {}, {}
-        for h in range(HALVES):
-            sums[h] = keep.tile([P, CHUNKS], F32, name=f"sums{h}")
-            shift[h] = keep.tile([P, CHUNKS], F32, name=f"shift{h}")
-            inv_mean[h] = keep.tile([P, 1], F32, name=f"inv_mean{h}")
-        last = keep.tile([P, 8 + P], F32)
-        neg_max[0] = last[:, 6:10]
-        stats = keep.tile([P, 2 * CHUNKS], F32)
-        neg_max[1] = stats[:, 0:4]
-        sums[0] = stats[:, 3:7]
-        sums[1] = sums[1][:]
-        mean[1] = keep.tile([P, 1], F32, name="mean1")[:]
-        mean[0] = keep.tile([P, 1], F32, name="mean0")[:]
+        neg_s = {}
 
-        def exponentials(h, chunks):
-            for j in chunks:
-                neg_s = keep.tile([P, N_TILE], F32, name=f"neg_s{h}_{j}")
-                nc.vector.tensor_scalar(neg_s[:], banks[h, j][:], neg_inv_temp[:, h : h + 1], None, ALU.mult, ALU.min, accum_out=neg_max[h][:, j : j + 1])
-                if j == CHUNKS - 1:
-                    neg_row_max = keep.tile([P, 1], F32, name=f"neg_row_max{h}")
-                    if h == 0:
-                        partial = keep.tile([P, 1], F32)
-                        nc.gpsimd.tensor_scalar(partial[:], neg_max[h][:, 0:1], neg_max[h][:, 1:2], neg_max[h][:, 2:3], ALU.min, ALU.min)
-                        nc.gpsimd.tensor_scalar(neg_row_max[:], partial[:], neg_max[h][:, 3:4], None, ALU.min)
-                    else:
-                        nc.vector.tensor_reduce(neg_row_max[:], neg_max[h], AX.X, ALU.min)
-                    nc.scalar.activation(shift[h][:], neg_max[h], ACT.Exp, bias=neg_row_max[:], scale=-1.0)
-                prob[h, j] = keep.tile([P, N_TILE], F32, name=f"prob{h}_{j}")
-                nc.scalar.activation(prob[h, j][:], neg_s[:], ACT.Exp, bias=neg_max[h][:, j : j + 1], scale=-1.0, accum_out=sums[h][:, j : j + 1])
+        def maxima(h, i):
+            neg_s[h, i] = keep.tile([P, PIECES[h][i][1]], F32, name=f"neg_s{h}_{i}")
+            nc.vector.tensor_scalar(neg_s[h, i][:], banks[h, i], neg_inv_temp[:, h : h + 1], None, ALU.mult, ALU.min, accum_out=neg_max[h][:, i : i + 1])
+
+        def exponential(h, i):
+            prob[h, i] = keep.tile([P, PIECES[h][i][1]], F32, name=f"prob{h}_{i}")
+            nc.scalar.activation(prob[h, i][:], neg_s[h, i][:], ACT.Exp, bias=neg_max[h][:, i : i + 1], scale=-1.0, accum_out=sums[h][:, i : i + 1])
+
+        def exponentials(h, pieces):
+            for i in pieces:
+                maxima(h, i)
+                exponential(h, i)
+
+        def shifts(h):
+            nc.scalar.activation(shift[h][:], neg_max[h], ACT.Exp, bias=neg_row_max[h], scale=-1.0)
 
         def normaliser(h):
-            weighted = keep.tile([P, CHUNKS], F32, name=f"weighted{h}")
-            nc.vector.scalar_tensor_tensor(weighted[:], sums[h], 1.0 / V, shift[h][:], ALU.mult, ALU.mult, accum_out=mean[h])
-            nc.vector.reciprocal(inv_mean[h][:], mean[h])
+            weighted = keep.tile([P, len(PIECES[h])], F32, name=f"weighted{h}")
+            nc.vector.scalar_tensor_tensor(weighted[:], sums[h], 1.0 / V, shift[h][:], ALU.mult, ALU.mult, accum_out=mean[h][:])
+            nc.vector.reciprocal(inv_mean[h][:], mean[h][:])
 
-        def emit(h, j, engine, pieces):
-            result = keep.tile([P, N_TILE], F32, name=f"result{h}_{j}")
-            for a, b in pieces:
-                engine.tensor_scalar(result[:, a:b], prob[h, j][:, a:b], shift[h][:, j : j + 1], inv_mean[h][:], ALU.mult, ALU.mult)
-                nc.sync.dma_start(out[h * P : (h + 1) * P, j * N_TILE + a : j * N_TILE + b], result[:, a:b])
+        result = [keep.tile([P, V], F32, name=f"result{h}") for h in range(HALVES)]
+
+        def emit(h, pieces, engine):
+            for i in pieces:
+                start, width = PIECES[h][i]
+                engine.tensor_scalar(result[h][:, start : start + width], prob[h, i][:], shift[h][:, i : i + 1], inv_mean[h][:], ALU.mult, ALU.mult)
+            a, b = PIECES[h][pieces[0]][0], sum(PIECES[h][pieces[-1]])
+            nc.sync.dma_start(out[h * P : (h + 1) * P, a:b], result[h][:, a:b])
 
         row = keep.tile([P, 3 * P], F32)
         diff0 = row[:, P : 2 * P]
@@ -147,7 +147,7 @@ def tile_attend_analogies_kernel(tc, ent, fsc, cand_words, cand_scales, temp, of
             less(t, 0, picked[0], diff0)
             if t < PACK - 1:
                 less(t, 1, picked[1], held[t])
-            sought = fresh(t, 0)
+            sought = keep.tile([P, P], F32, name=f"sought{t}")[:]
             finish(t, 0, diff0, sought)
         score(0)
         finish(0, 1, held[0], picked[0])
@@ -155,17 +155,26 @@ def tile_attend_analogies_kernel(tc, ent, fsc, cand_words, cand_scales, temp, of
         pick(3, 1, row[:, 2 * P - 8 : 3 * P - 8])
         less(3, 1, row[:, 2 * P - 8 : 3 * P - 8], sought)
         finish(2, 1, held[2], grouped[0][:].rearrange("p q t -> p (q t)").bitcast(F32)[:, :P])
-        finish(3, 1, sought, last[:, 8:])
-        exponentials(0, range(1))
+        finish(3, 1, sought, last)
+
+        exponentials(0, range(2))
         score(1)
-        exponentials(0, range(1, CHUNKS))
+        exponentials(0, range(2, NP))
+        partial = sums[1][:, 0:1]
+        nc.gpsimd.tensor_scalar(partial, neg_max[0][:, 0:1], neg_max[0][:, 1:2], neg_max[0][:, 2:3], ALU.min, ALU.min)
+        nc.gpsimd.tensor_scalar(neg_row_max[0], partial, neg_max[0][:, 3:4], neg_max[0][:, 4:5], ALU.min, ALU.min)
+        shifts(0)
         exponentials(1, range(2))
         normaliser(0)
-        emit(0, 0, nc.gpsimd, [(0, 128), (128, N_TILE)])
-        emit(0, 1, nc.gpsimd, [(0, N_TILE)])
-        exponentials(1, range(2, CHUNKS))
-        emit(0, 2, nc.vector, [(0, N_TILE)])
-        emit(0, 3, nc.vector, [(0, N_TILE)])
+        emit(0, (0,), nc.gpsimd)
+        emit(0, (1,), nc.gpsimd)
+        exponentials(1, (2,))
+        maxima(1, 3)
+        nc.vector.tensor_reduce(neg_row_max[1], neg_max[1], AX.X, ALU.min)
+        shifts(1)
+        exponential(1, 3)
+        emit(0, (2,), nc.vector)
+        emit(0, (3, 4), nc.vector)
         normaliser(1)
-        for j in range(CHUNKS):
-            emit(1, j, nc.vector, [(0, N_TILE)])
+        for pieces in ((0,), (1,), (2, 3)):
+            emit(1, pieces, nc.vector)

@@ -19,14 +19,12 @@ AX = mybir.AxisListType
 P = 128
 PACK = 4
 HALVES = Q // P
-N_TILE = 512
-CHUNKS = V // N_TILE
-LIST_COLS = P // 16
-PIECES = (
-    ((0, 256), (256, 256), (512, 512), (1024, 512), (1536, 512)),
-    ((0, 512), (512, 512), (1024, 512), (1536, 512)),
-)
-NP = 5
+CHUNK = 512
+CHUNKS = V // CHUNK
+STRIPE = 16
+QUADRANTS = 4
+LOWEST = -3.4028234663852886e38
+LAP = 8
 
 
 def tile_attend_analogies_kernel(tc, ent, fsc, cand_words, cand_scales, temp, offs, offs2, offs3, out):
@@ -36,12 +34,12 @@ def tile_attend_analogies_kernel(tc, ent, fsc, cand_words, cand_scales, temp, of
         psum = ctx.enter_context(tc.psum_pool(name="psum", bufs=1))
 
         planes = [keep.tile([P, T], F32, name=f"plane{t}") for t in range(PACK)]
-        first = keep.tile([P, Q // 16], U16)
-        second = keep.tile([P, Q // 16], U16)
-        third = keep.tile([P, Q // 16], U16)
+        first = keep.tile([P, Q // STRIPE], U16)
+        second = keep.tile([P, Q // STRIPE], U16)
+        third = keep.tile([P, Q // STRIPE], U16)
         fsc_sb = keep.tile([P, PACK], F32)
         temp_sb = keep.tile([P, HALVES], F32)
-        cand_plane = keep.tile([P, N_TILE], U8, align_bytes=64)
+        cand_plane = keep.tile([P, CHUNK], U8, align_bytes=64)
         cand_sb = keep.tile([P, V], U32, align_bytes=64)
 
         ent_planes = ent.rearrange("(p t) c -> t p c", t=PACK)
@@ -58,123 +56,124 @@ def tile_attend_analogies_kernel(tc, ent, fsc, cand_words, cand_scales, temp, of
         with nc.allow_non_contiguous_dma(reason="one temperature a partition and half"):
             nc.gpsimd.dma_start(temp_sb[:], temp.rearrange("(h p) o -> p (h o)", p=P))
         scale_words = cand_scales[0].bitcast(I32).rearrange("f (j c) -> j f c", j=CHUNKS)
-        for g in range(4):
-            nc.gpsimd.dma_start(cand_plane[32 * g : 32 * g + 16, :].bitcast(I32), scale_words[:, 4 * g : 4 * g + 4, :])
+        for g in range(QUADRANTS):
+            nc.gpsimd.dma_start(cand_plane[32 * g : 32 * g + 4 * CHUNKS, :].bitcast(I32), scale_words[:, 4 * g : 4 * g + 4, :])
+
         neg_temp = keep.tile([P, HALVES], F32)
         nc.gpsimd.tensor_scalar(neg_temp[:], temp_sb[:], -1.0, 0.0, ALU.mult, ALU.add)
         neg_inv_temp = keep.tile([P, HALVES], F32)
         nc.vector.reciprocal(neg_inv_temp[:], neg_temp[:])
 
-        warm = keep.tile([P, 1], F32)
-        nc.vector.memset(warm[:], 0.0)
-        warm_out = keep.tile([P, 1], F32)
-        nc.scalar.activation(warm_out[:], warm[:], ACT.Exp)
-
-        picked = [keep.tile([P, P], F32, name=f"picked{lane}")[:] for lane in range(2)]
-        stats = keep.tile([P, 2 * NP], F32)
-        mixed = keep.tile([P, 2 * P + 8], F32)
+        picked = [keep.tile([P, P], F32, name=f"picked{h}")[:] for h in range(HALVES)]
+        stats = keep.tile([P, 2 * CHUNKS], F32)
+        mixed = keep.tile([P, 2 * P + LAP], F32)
         held = [keep.tile([P, P], F32, name=f"held{t}")[:] for t in range(2)] + [mixed[:, :P]]
-        last = mixed[:, P + 8 :]
-        neg_max = [mixed[:, P - 1 : P + 20 : 5], stats[:, 0:CHUNKS]]
+        last_sought = mixed[:, P + LAP :]
+        neg_max = [mixed[:, P - 1 : P + 15 : 5], stats[:, 0:CHUNKS]]
+        sums = [stats[:, 2 : 2 + CHUNKS], keep.tile([P, CHUNKS], F32, name="sums1")[:]]
         grouped = [keep.tile([P, P, PACK], BF16, name=f"grouped{h}", align_bytes=64) for h in range(HALVES)]
         codes = [keep.tile([P, P], U32, name=f"codes{h}", align_bytes=64) for h in range(HALVES)]
         sv_plane = [keep.tile([P, P], U8, name=f"sv_plane{h}", align_bytes=64) for h in range(HALVES)]
-        sums = [stats[:, 2 : 2 + NP], keep.tile([P, CHUNKS], F32, name="sums1")[:]]
-        shift = [keep.tile([P, len(PIECES[h])], F32, name=f"shift{h}") for h in range(HALVES)]
-        mean = [keep.tile([P, 1], F32, name=f"mean{h}") for h in range(HALVES)]
+        banks = [[psum.tile([P, CHUNK], F32, name=f"bank{h}_{j}") for j in range(CHUNKS)] for h in range(HALVES)]
+        neg_s = [[keep.tile([P, CHUNK], F32, name=f"neg_s{h}_{j}") for j in range(CHUNKS)] for h in range(HALVES)]
+        prob = [keep.tile([P, V], F32, name=f"prob{h}") for h in range(HALVES)]
+        result = [keep.tile([P, V], F32, name=f"result{h}") for h in range(HALVES)]
+        neg_row_max = [keep.tile([P, 1], F32, name=f"neg_row_max{h}") for h in range(HALVES)]
+        shift = [keep.tile([P, CHUNKS], F32, name=f"shift{h}") for h in range(HALVES)]
         inv_mean = [keep.tile([P, 1], F32, name=f"inv_mean{h}") for h in range(HALVES)]
-        neg_row_max = [keep.tile([P, 1], F32, name=f"neg_row_max{h}")[:] for h in range(HALVES)]
-        cols = [slice(h * LIST_COLS, (h + 1) * LIST_COLS) for h in range(HALVES)]
-        banks, prob = {}, {}
+        list_cols = [slice(h * P // STRIPE, (h + 1) * P // STRIPE) for h in range(HALVES)]
+        chunk_cols = [slice(j * CHUNK, (j + 1) * CHUNK) for j in range(CHUNKS)]
 
         def pick(t, h, dst):
-            nc.vector.tensor_copy(dst, planes[t][:].indirect(second[:, cols[h]]))
+            nc.vector.tensor_copy(dst, planes[t][:].indirect(second[:, list_cols[h]]))
 
         def less(t, h, src, dst):
-            nc.vector.tensor_tensor(dst, planes[t][:].indirect(first[:, cols[h]]), src, ALU.subtract)
+            nc.vector.tensor_tensor(dst, planes[t][:].indirect(first[:, list_cols[h]]), src, ALU.subtract)
 
         def finish(t, h, src, dst):
-            nc.vector.tensor_tensor(dst, planes[t][:].indirect(third[:, cols[h]]), src, ALU.subtract)
+            nc.vector.tensor_tensor(dst, planes[t][:].indirect(third[:, list_cols[h]]), src, ALU.subtract)
             nc.scalar.activation(grouped[h][:, :, t], dst, ACT.Copy, scale=fsc_sb[:, t : t + 1])
 
         def score(h):
             nc.vector.quantize_mx(out=codes[h][:].bitcast(FP8X4), scales=sv_plane[h][:], in_=grouped[h][:].rearrange("p q t -> p (q t)"))
-            whole = [psum.tile([P, N_TILE], F32, name=f"bank{h}_{j}") for j in range(CHUNKS)]
-            for i, (start, width) in enumerate(PIECES[h]):
-                j, a = divmod(start, N_TILE)
-                banks[h, i] = whole[j][:, a : a + width]
-                nc.tensor.matmul_mx(out=banks[h, i], lhsT=codes[h][:].bitcast(FP8X4), lhsT_scale=sv_plane[h][:],
-                                    rhs=cand_sb[:, start : start + width].bitcast(FP8X4), rhs_scale=cand_plane[4 * j : P, a : a + width], start=True, stop=True)
+            for j in range(CHUNKS):
+                nc.tensor.matmul_mx(
+                    out=banks[h][j][:],
+                    lhsT=codes[h][:].bitcast(FP8X4),
+                    lhsT_scale=sv_plane[h][:],
+                    rhs=cand_sb[:, chunk_cols[j]].bitcast(FP8X4),
+                    rhs_scale=cand_plane[4 * j : P, :],
+                    start=True,
+                    stop=True,
+                )
 
-        neg_s = {}
+        def chunk_max(h, j):
+            nc.vector.tensor_scalar(neg_s[h][j][:], banks[h][j][:], neg_inv_temp[:, h : h + 1], None, ALU.mult, ALU.min, accum_out=neg_max[h][:, j : j + 1])
 
-        def maxima(h, i):
-            neg_s[h, i] = keep.tile([P, PIECES[h][i][1]], F32, name=f"neg_s{h}_{i}")
-            nc.vector.tensor_scalar(neg_s[h, i][:], banks[h, i], neg_inv_temp[:, h : h + 1], None, ALU.mult, ALU.min, accum_out=neg_max[h][:, i : i + 1])
-
-        def exponential(h, i):
-            prob[h, i] = keep.tile([P, PIECES[h][i][1]], F32, name=f"prob{h}_{i}")
-            nc.scalar.activation(prob[h, i][:], neg_s[h, i][:], ACT.Exp, bias=neg_max[h][:, i : i + 1], scale=-1.0, accum_out=sums[h][:, i : i + 1])
-
-        def exponentials(h, pieces):
-            for i in pieces:
-                maxima(h, i)
-                exponential(h, i)
+        def chunk_exp(h, j):
+            nc.scalar.activation(prob[h][:, chunk_cols[j]], neg_s[h][j][:], ACT.Exp, bias=neg_max[h][:, j : j + 1], scale=-1.0, accum_out=sums[h][:, j : j + 1])
 
         def shifts(h):
-            nc.scalar.activation(shift[h][:], neg_max[h], ACT.Exp, bias=neg_row_max[h], scale=-1.0)
+            nc.scalar.activation(shift[h][:], neg_max[h], ACT.Exp, bias=neg_row_max[h][:], scale=-1.0)
 
         def normaliser(h):
-            weighted = keep.tile([P, len(PIECES[h])], F32, name=f"weighted{h}")
-            nc.vector.scalar_tensor_tensor(weighted[:], sums[h], 1.0 / V, shift[h][:], ALU.mult, ALU.mult, accum_out=mean[h][:])
-            nc.vector.reciprocal(inv_mean[h][:], mean[h][:])
+            weighted = keep.tile([P, CHUNKS], F32, name=f"weighted{h}")
+            mean = keep.tile([P, 1], F32, name=f"mean{h}")
+            nc.vector.scalar_tensor_tensor(weighted[:], sums[h], 1.0 / V, shift[h][:], ALU.mult, ALU.mult, accum_out=mean[:])
+            nc.vector.reciprocal(inv_mean[h][:], mean[:])
 
-        result = [keep.tile([P, V], F32, name=f"result{h}") for h in range(HALVES)]
-
-        def emit(h, pieces, engine):
-            for i in pieces:
-                start, width = PIECES[h][i]
-                engine.tensor_scalar(result[h][:, start : start + width], prob[h, i][:], shift[h][:, i : i + 1], inv_mean[h][:], ALU.mult, ALU.mult)
-            a, b = PIECES[h][pieces[0]][0], sum(PIECES[h][pieces[-1]])
-            nc.sync.dma_start(out[h * P : (h + 1) * P, a:b], result[h][:, a:b])
+        def emit(h, start, stop, engine):
+            for a in range(start, stop, CHUNK):
+                cols = slice(a, min(a + CHUNK, stop))
+                j = a // CHUNK
+                engine.tensor_scalar(result[h][:, cols], prob[h][:, cols], shift[h][:, j : j + 1], inv_mean[h][:], ALU.mult, ALU.mult)
+            nc.sync.dma_start(out[h * P : (h + 1) * P, start:stop], result[h][:, start:stop])
 
         row = keep.tile([P, 3 * P], F32)
-        diff0 = row[:, P : 2 * P]
+        diff = row[:, P : 2 * P]
         for t in range(PACK):
             pick(t, 0, picked[0])
             if t < PACK - 1:
                 pick(t, 1, picked[1])
-            less(t, 0, picked[0], diff0)
+            less(t, 0, picked[0], diff)
             if t < PACK - 1:
                 less(t, 1, picked[1], held[t])
             sought = keep.tile([P, P], F32, name=f"sought{t}")[:]
-            finish(t, 0, diff0, sought)
+            finish(t, 0, diff, sought)
         score(0)
         finish(0, 1, held[0], picked[0])
-        finish(1, 1, held[1], row[:, 8 : P + 8])
-        pick(3, 1, row[:, 2 * P - 8 : 3 * P - 8])
-        less(3, 1, row[:, 2 * P - 8 : 3 * P - 8], sought)
+        finish(1, 1, held[1], row[:, LAP : P + LAP])
+        pick(3, 1, row[:, 2 * P - LAP : 3 * P - LAP])
+        less(3, 1, row[:, 2 * P - LAP : 3 * P - LAP], sought)
         finish(2, 1, held[2], grouped[0][:].rearrange("p q t -> p (q t)").bitcast(F32)[:, :P])
-        finish(3, 1, sought, last)
+        finish(3, 1, sought, last_sought)
 
-        exponentials(0, range(2))
-        score(1)
-        exponentials(0, range(2, NP))
+        for j in range(CHUNKS):
+            if j == CHUNKS // 2:
+                score(1)
+            chunk_max(0, j)
+            chunk_exp(0, j)
+        pair = keep.tile([P, 1], F32)
         partial = sums[1][:, 0:1]
-        nc.gpsimd.tensor_scalar(partial, neg_max[0][:, 0:1], neg_max[0][:, 1:2], neg_max[0][:, 2:3], ALU.min, ALU.min)
-        nc.gpsimd.tensor_scalar(neg_row_max[0], partial, neg_max[0][:, 3:4], neg_max[0][:, 4:5], ALU.min, ALU.min)
+        for dst, src, j in ((pair[:], neg_max[0][:, 0:1], 1), (partial, pair[:], 2), (neg_row_max[0][:], partial, 3)):
+            nc.gpsimd.tensor_scalar(dst, src, neg_max[0][:, j : j + 1], LOWEST, ALU.min, ALU.max)
         shifts(0)
-        exponentials(1, range(2))
+
+        for j in range(CHUNKS // 2):
+            chunk_max(1, j)
+            chunk_exp(1, j)
         normaliser(0)
-        emit(0, (0,), nc.gpsimd)
-        emit(0, (1,), nc.gpsimd)
-        exponentials(1, (2,))
-        maxima(1, 3)
-        nc.vector.tensor_reduce(neg_row_max[1], neg_max[1], AX.X, ALU.min)
+        emit(0, 0, CHUNK // 2, nc.gpsimd)
+        emit(0, CHUNK // 2, CHUNK, nc.gpsimd)
+        chunk_max(1, 2)
+        chunk_exp(1, 2)
+        chunk_max(1, 3)
+        nc.vector.tensor_reduce(neg_row_max[1][:], neg_max[1], AX.X, ALU.min)
         shifts(1)
-        exponential(1, 3)
-        emit(0, (2,), nc.vector)
-        emit(0, (3, 4), nc.vector)
+        chunk_exp(1, 3)
+        emit(0, CHUNK, 2 * CHUNK, nc.vector)
+        emit(0, 2 * CHUNK, V, nc.vector)
         normaliser(1)
-        for pieces in ((0,), (1,), (2, 3)):
-            emit(1, pieces, nc.vector)
+        emit(1, 0, CHUNK, nc.vector)
+        emit(1, CHUNK, 2 * CHUNK, nc.vector)
+        emit(1, 2 * CHUNK, V, nc.vector)

from contextlib import ExitStack

import concourse.mybir as mybir

D, T, Q, V = 512, 1024, 256, 2048
FLOPS = 2 * D * Q * V

F32 = mybir.dt.float32
BF16 = mybir.dt.bfloat16
I32 = mybir.dt.int32
U32 = mybir.dt.uint32
U16 = mybir.dt.uint16
U8 = mybir.dt.uint8
FP8X4 = mybir.dt.float8_e4m3fn_x4
ALU = mybir.AluOpType
ACT = mybir.ActivationFunctionType
AX = mybir.AxisListType

P = 128
PACK = 4
HALVES = Q // P
CHUNK = 512
CHUNKS = V // CHUNK
STRIPE = 16
QUADRANTS = 4
LOWEST = -3.4028234663852886e38
LAP = 8


def tile_attend_analogies_kernel(tc, ent, fsc, cand_words, cand_scales, temp, offs, offs2, offs3, out):
    nc = tc.nc
    with ExitStack() as ctx:
        keep = ctx.enter_context(tc.tile_pool(name="keep", bufs=1))
        psum = ctx.enter_context(tc.psum_pool(name="psum", bufs=1))

        planes = [keep.tile([P, T], F32, name=f"plane{t}") for t in range(PACK)]
        first = keep.tile([P, Q // STRIPE], U16)
        second = keep.tile([P, Q // STRIPE], U16)
        third = keep.tile([P, Q // STRIPE], U16)
        fsc_sb = keep.tile([P, PACK], F32)
        temp_sb = keep.tile([P, HALVES], F32)
        cand_plane = keep.tile([P, CHUNK], U8, align_bytes=64)
        cand_sb = keep.tile([P, V], U32, align_bytes=64)

        ent_planes = ent.rearrange("(p t) c -> t p c", t=PACK)
        nc.vector.memset(cand_plane[:].bitcast(I32), 0)
        nc.sync.dma_start(planes[0][:], ent_planes[0])
        nc.sync.dma_start(second[:], offs2)
        nc.sync.dma_start(first[:], offs)
        nc.sync.dma_start(third[:], offs3)
        nc.sync.dma_start(planes[1][:], ent_planes[1])
        nc.sync.dma_start(fsc_sb[:], fsc.rearrange("(p t) o -> p (t o)", t=PACK))
        nc.sync.dma_start(planes[2][:], ent_planes[2])
        nc.sync.dma_start(planes[3][:], ent_planes[3])
        nc.sync.dma_start(cand_sb[:].bitcast(I32), cand_words[0].rearrange("p n t -> p (n t)").bitcast(I32))
        with nc.allow_non_contiguous_dma(reason="one temperature a partition and half"):
            nc.gpsimd.dma_start(temp_sb[:], temp.rearrange("(h p) o -> p (h o)", p=P))
        scale_words = cand_scales[0].bitcast(I32).rearrange("f (j c) -> j f c", j=CHUNKS)
        for g in range(QUADRANTS):
            nc.gpsimd.dma_start(cand_plane[32 * g : 32 * g + 4 * CHUNKS, :].bitcast(I32), scale_words[:, 4 * g : 4 * g + 4, :])

        neg_temp = keep.tile([P, HALVES], F32)
        nc.gpsimd.tensor_scalar(neg_temp[:], temp_sb[:], -1.0, 0.0, ALU.mult, ALU.add)
        neg_inv_temp = keep.tile([P, HALVES], F32)
        nc.vector.reciprocal(neg_inv_temp[:], neg_temp[:])

        picked = [keep.tile([P, P], F32, name=f"picked{h}")[:] for h in range(HALVES)]
        stats = keep.tile([P, 2 * CHUNKS], F32)
        mixed = keep.tile([P, 2 * P + LAP], F32)
        held = [keep.tile([P, P], F32, name=f"held{t}")[:] for t in range(2)] + [mixed[:, :P]]
        last_sought = mixed[:, P + LAP :]
        neg_max = [mixed[:, P - 1 : P + 15 : 5], stats[:, 0:CHUNKS]]
        sums = [stats[:, 2 : 2 + CHUNKS], keep.tile([P, CHUNKS], F32, name="sums1")[:]]
        grouped = [keep.tile([P, P, PACK], BF16, name=f"grouped{h}", align_bytes=64) for h in range(HALVES)]
        codes = [keep.tile([P, P], U32, name=f"codes{h}", align_bytes=64) for h in range(HALVES)]
        sv_plane = [keep.tile([P, P], U8, name=f"sv_plane{h}", align_bytes=64) for h in range(HALVES)]
        banks = [[psum.tile([P, CHUNK], F32, name=f"bank{h}_{j}") for j in range(CHUNKS)] for h in range(HALVES)]
        neg_s = [[keep.tile([P, CHUNK], F32, name=f"neg_s{h}_{j}") for j in range(CHUNKS)] for h in range(HALVES)]
        prob = [keep.tile([P, V], F32, name=f"prob{h}") for h in range(HALVES)]
        result = [keep.tile([P, V], F32, name=f"result{h}") for h in range(HALVES)]
        neg_row_max = [keep.tile([P, 1], F32, name=f"neg_row_max{h}") for h in range(HALVES)]
        shift = [keep.tile([P, CHUNKS], F32, name=f"shift{h}") for h in range(HALVES)]
        inv_mean = [keep.tile([P, 1], F32, name=f"inv_mean{h}") for h in range(HALVES)]
        list_cols = [slice(h * P // STRIPE, (h + 1) * P // STRIPE) for h in range(HALVES)]
        chunk_cols = [slice(j * CHUNK, (j + 1) * CHUNK) for j in range(CHUNKS)]

        def pick(t, h, dst):
            nc.vector.tensor_copy(dst, planes[t][:].indirect(second[:, list_cols[h]]))

        def less(t, h, src, dst):
            nc.vector.tensor_tensor(dst, planes[t][:].indirect(first[:, list_cols[h]]), src, ALU.subtract)

        def finish(t, h, src, dst):
            nc.vector.tensor_tensor(dst, planes[t][:].indirect(third[:, list_cols[h]]), src, ALU.subtract)
            nc.scalar.activation(grouped[h][:, :, t], dst, ACT.Copy, scale=fsc_sb[:, t : t + 1])

        def score(h):
            nc.vector.quantize_mx(out=codes[h][:].bitcast(FP8X4), scales=sv_plane[h][:], in_=grouped[h][:].rearrange("p q t -> p (q t)"))
            for j in range(CHUNKS):
                nc.tensor.matmul_mx(
                    out=banks[h][j][:],
                    lhsT=codes[h][:].bitcast(FP8X4),
                    lhsT_scale=sv_plane[h][:],
                    rhs=cand_sb[:, chunk_cols[j]].bitcast(FP8X4),
                    rhs_scale=cand_plane[4 * j : P, :],
                    start=True,
                    stop=True,
                )

        def chunk_max(h, j):
            nc.vector.tensor_scalar(neg_s[h][j][:], banks[h][j][:], neg_inv_temp[:, h : h + 1], None, ALU.mult, ALU.min, accum_out=neg_max[h][:, j : j + 1])

        def chunk_exp(h, j):
            nc.scalar.activation(prob[h][:, chunk_cols[j]], neg_s[h][j][:], ACT.Exp, bias=neg_max[h][:, j : j + 1], scale=-1.0, accum_out=sums[h][:, j : j + 1])

        def shifts(h):
            nc.scalar.activation(shift[h][:], neg_max[h], ACT.Exp, bias=neg_row_max[h][:], scale=-1.0)

        def normaliser(h):
            weighted = keep.tile([P, CHUNKS], F32, name=f"weighted{h}")
            mean = keep.tile([P, 1], F32, name=f"mean{h}")
            nc.vector.scalar_tensor_tensor(weighted[:], sums[h], 1.0 / V, shift[h][:], ALU.mult, ALU.mult, accum_out=mean[:])
            nc.vector.reciprocal(inv_mean[h][:], mean[:])

        def emit(h, start, stop, engine):
            for a in range(start, stop, CHUNK):
                cols = slice(a, min(a + CHUNK, stop))
                j = a // CHUNK
                engine.tensor_scalar(result[h][:, cols], prob[h][:, cols], shift[h][:, j : j + 1], inv_mean[h][:], ALU.mult, ALU.mult)
            nc.sync.dma_start(out[h * P : (h + 1) * P, start:stop], result[h][:, start:stop])

        row = keep.tile([P, 3 * P], F32)
        diff = row[:, P : 2 * P]
        for t in range(PACK):
            pick(t, 0, picked[0])
            if t < PACK - 1:
                pick(t, 1, picked[1])
            less(t, 0, picked[0], diff)
            if t < PACK - 1:
                less(t, 1, picked[1], held[t])
            sought = keep.tile([P, P], F32, name=f"sought{t}")[:]
            finish(t, 0, diff, sought)
        score(0)
        finish(0, 1, held[0], picked[0])
        finish(1, 1, held[1], row[:, LAP : P + LAP])
        pick(3, 1, row[:, 2 * P - LAP : 3 * P - LAP])
        less(3, 1, row[:, 2 * P - LAP : 3 * P - LAP], sought)
        finish(2, 1, held[2], grouped[0][:].rearrange("p q t -> p (q t)").bitcast(F32)[:, :P])
        finish(3, 1, sought, last_sought)

        for j in range(CHUNKS):
            if j == CHUNKS // 2:
                score(1)
            chunk_max(0, j)
            chunk_exp(0, j)
        pair = keep.tile([P, 1], F32)
        partial = sums[1][:, 0:1]
        for dst, src, j in ((pair[:], neg_max[0][:, 0:1], 1), (partial, pair[:], 2), (neg_row_max[0][:], partial, 3)):
            nc.gpsimd.tensor_scalar(dst, src, neg_max[0][:, j : j + 1], LOWEST, ALU.min, ALU.max)
        shifts(0)

        for j in range(CHUNKS // 2):
            chunk_max(1, j)
            chunk_exp(1, j)
        normaliser(0)
        emit(0, 0, CHUNK // 2, nc.gpsimd)
        emit(0, CHUNK // 2, CHUNK, nc.gpsimd)
        chunk_max(1, 2)
        chunk_exp(1, 2)
        chunk_max(1, 3)
        nc.vector.tensor_reduce(neg_row_max[1][:], neg_max[1], AX.X, ALU.min)
        shifts(1)
        chunk_exp(1, 3)
        emit(0, CHUNK, 2 * CHUNK, nc.vector)
        emit(0, 2 * CHUNK, V, nc.vector)
        normaliser(1)
        emit(1, 0, CHUNK, nc.vector)
        emit(1, CHUNK, 2 * CHUNK, nc.vector)
        emit(1, 2 * CHUNK, V, nc.vector)
